import numpy as np
import ml_dtypes


def mxq(x, axis, fmt="e4m3"):
    dtype, down = {"e4m3": (ml_dtypes.float8_e4m3fn, 7), "e5m2": (ml_dtypes.float8_e5m2, 14)}[fmt]
    v = np.moveaxis(np.asarray(x, np.float32).astype(ml_dtypes.bfloat16).astype(np.float64), axis, -1)
    blocks = v.reshape(v.shape[:-1] + (-1, 32))
    amax = np.abs(blocks).max(-1, keepdims=True)
    byte = np.maximum(np.where(amax > 0, np.frexp(amax)[1] - 1 + 127, 0) - down, 1)
    scale = np.exp2(byte - 127.0)
    codes = (blocks / scale).astype(np.float32).astype(dtype).astype(np.float64)
    return np.moveaxis((codes * scale).reshape(v.shape), -1, axis)


WIDE = False


def mx_kscale(k):
    if not WIDE:
        return np.ones(k)
    levels = np.array([30, -30])
    if k % 512:
        return np.exp2(np.random.permutation(np.resize(levels, k // 32))).repeat(32)
    a = np.empty((k // 512, 16))
    for p in range(k // 512):
        a[p, :8] = np.random.permutation(np.resize(levels, 8))
        for g in range(8):
            far = levels[np.abs(levels - a[p, g]) >= 10]
            a[p, g + 8] = far[np.random.randint(len(far))]
    return np.exp2(a.ravel()).repeat(32)


def f64(x):
    return np.asarray(x).astype(np.float64)


def striped(idx):
    return np.tile(np.asarray(idx).reshape(-1, 16).T, (8, 1)).astype(np.uint16)


def unstriped(offs):
    return offs[:16].T.reshape(-1).astype(np.int64)


E2M1 = np.array([0.0, 0.5, 1.0, 1.5, 2.0, 3.0, 4.0, 6.0, -0.0, -0.5, -1.0, -1.5, -2.0, -3.0, -4.0, -6.0])


def pack_weight(w, fmt):
    k, n = w.shape
    w = f64(np.asarray(w, np.float32).astype(ml_dtypes.bfloat16)).reshape(k // 32, 32, n)
    amax = np.abs(w).max(1)
    if fmt == "e4m3":
        byte = np.frexp(amax)[1] - 1 + 127 - 7
    else:
        mant, ex = np.frexp(amax / 6.0)
        byte = np.where(mant > 0.5, ex, ex - 1) + 127
    byte = np.clip(np.where(amax > 0, byte, 1), 1, 254)
    scaled = (w * np.exp2(127.0 - byte)[:, None, :]).reshape(k, n).astype(np.float32)
    by_word = np.ascontiguousarray(scaled.reshape(k // 512, 128, 4, n).transpose(0, 1, 3, 2))
    if fmt == "e4m3":
        words = by_word.astype(ml_dtypes.float8_e4m3fn).view(np.uint8)
    else:
        c = by_word.astype(ml_dtypes.float4_e2m1fn).view(np.uint8) & 0xF
        words = (c[..., 0::2] | (c[..., 1::2] << 4)).reshape(k // 512, 128, 2 * n)
    return np.ascontiguousarray(words), np.ascontiguousarray(byte.astype(np.uint8).reshape(k // 512, 16, n))


def unpack_weight(words, scales, fmt):
    g, _, n = scales.shape
    words = np.ascontiguousarray(words).reshape(g, 128, n, -1)
    if fmt == "e4m3":
        vals = words.view(ml_dtypes.float8_e4m3fn).astype(np.float64)
    else:
        nib = np.empty((g, 128, n, 4), np.uint8)
        nib[..., 0::2] = words & 0xF
        nib[..., 1::2] = words >> 4
        vals = E2M1[nib]
    vals = vals * np.repeat(np.exp2(scales.astype(np.float64) - 127.0), 8, axis=1)[..., None]
    return vals.transpose(0, 1, 3, 2).reshape(g * 512, n)


K, T, J, R, X, O, N, E = 512, 1024, 256, 512, 1024, 128, 256, 512


def setup_inputs():
    n = np.random.standard_normal
    idx = np.random.permutation(T)[:J]
    idx2 = np.random.permutation(J)[:O]
    idx3 = np.random.permutation(X)[:O]
    idx4 = np.random.permutation(X)[:O]
    idx5 = np.random.permutation(T)[:O]
    idx6 = np.random.permutation(E)[:O]
    idx7 = np.random.permutation(E)[:O]
    fk = mx_kscale(K)
    fr = mx_kscale(R)
    xtp = pack_weight(n((K, T)) / fk[:, None], "e2m1")
    wp = pack_weight(n((K, R)) * 1 / np.sqrt(K) * fk[:, None] * fr, "e4m3")
    wbp = pack_weight(n((R, N)) * 1 / np.sqrt(R) / fr[:, None], "e2m1")
    wsp = pack_weight(n((K, N)) * 1 / np.sqrt(K) * fk[:, None], "e4m3")
    return {
        "xt_words": xtp[0],
        "xt_scales": xtp[1],
        "w_words": wp[0],
        "w_scales": wp[1],
        "tb": (n((R, X)) * 1.0).astype(np.float32),
        "wb_words": wbp[0],
        "wb_scales": wbp[1],
        "ws_words": wsp[0],
        "ws_scales": wsp[1],
        "offs": striped(idx),
        "offs2": striped(idx2),
        "offs3": striped(idx3),
        "offs4": striped(idx4),
        "offs5": striped(idx5),
        "offs6": striped(idx6),
        "offs7": striped(idx7),
    }


def reference(xt_words, xt_scales, w_words, w_scales, tb, wb_words, wb_scales, ws_words, ws_scales, offs, offs2, offs3, offs4, offs5, offs6, offs7):
    idx = unstriped(offs)
    idx2 = unstriped(offs2)
    idx3 = unstriped(offs3)
    idx4 = unstriped(offs4)
    idx5 = unstriped(offs5)
    idx6 = unstriped(offs6)
    idx7 = unstriped(offs7)
    xtu = unpack_weight(xt_words, xt_scales, "e2m1")
    wu = unpack_weight(w_words, w_scales, "e4m3")
    wbu = unpack_weight(wb_words, wb_scales, "e2m1")
    wsu = unpack_weight(ws_words, ws_scales, "e4m3")
    xtidxg = xtu[:, idx]
    a = wu.T @ xtidxg
    la = a[:, 0:1]
    la2 = a[:, 128:129]
    hid = np.maximum(np.minimum(a[:, idx2], f64(tb)[:, idx3] * la), f64(tb)[:, idx4] * la2)
    hidq = mxq(hid, 0, "e5m2")
    xtidx5g = xtu[:, idx5]
    p = wbu.T @ hidq + wsu.T @ xtidx5g
    pa = np.zeros((N, E))
    pa[:, idx6] = p
    pb = np.zeros((N, E))
    pb[:, idx7] = p
    y = pa + pb
    return y

@@ -1,0 +1,158 @@
+from contextlib import ExitStack
+
+import concourse.mybir as mybir
+
+K, T, J, R, X, O, N, E = 512, 1024, 256, 512, 1024, 128, 256, 512
+FLOPS = 2 * K * R * J + 2 * R * N * O + 2 * K * N * O
+
+F32 = mybir.dt.float32
+BF16 = mybir.dt.bfloat16
+I32 = mybir.dt.int32
+U32 = mybir.dt.uint32
+U16 = mybir.dt.uint16
+U8 = mybir.dt.uint8
+E4M3 = mybir.dt.float8_e4m3fn_x4
+E5M2 = mybir.dt.float8_e5m2_x4
+E2M1 = mybir.dt.float4_e2m1fn_x4
+COPY = mybir.ActivationFunctionType.Copy
+ALU = mybir.AluOpType
+
+P = 128
+PACK = 4
+LA_COL, LA2_COL = 0, 128
+
+
+def tile_list_leadbounds_solo_further_pagetwice_kernel(
+    tc, xt_words, xt_scales, w_words, w_scales, tb, wb_words, wb_scales, ws_words, ws_scales,
+    offs, offs2, offs3, offs4, offs5, offs6, offs7, out,
+):
+    nc = tc.nc
+    with ExitStack() as ctx:
+        sb = ctx.enter_context(tc.tile_pool(name="sb", bufs=1))
+        ps = ctx.enter_context(tc.psum_pool(name="ps", bufs=1))
+
+        def tile(name, shape, dtype):
+            return sb.tile(shape, dtype, name=name, align_bytes=64)
+
+        def load_list(name, src):
+            lst = tile(name, list(src.shape), U16)
+            nc.sync.dma_start(lst[:], src)
+            return lst
+
+        def load_scale_halves(queue, dst, src):
+            rows = src[0].bitcast(I32).rearrange("(h q r) c -> q r h c", h=2, q=2)
+            for q in range(2):
+                queue.dma_start(dst[32 * q : 32 * q + 4], rows[q])
+
+        xt_stage = tile("xt_stage", [64, 2, T // 4], I32)
+        w_stage = tile("w_stage", [P, 2, R // 4], I32)
+        out_stage = tile("out_stage", [P, 2, 2 * N // 4], I32)
+        nc.gpsimd.memset(xt_stage[:], 0)
+        nc.vector.memset(w_stage[:], 0)
+        nc.gpsimd.memset(out_stage[:], 0)
+        pages = [[tile(f"page{s}{h}", [P, E], F32) for h in range(2)] for s in range(2)]
+        for s in range(2):
+            for h in range(2):
+                nc.vector.memset(pages[s][h][:], 0.0)
+
+        xt_w = tile("xt_w", [P, T], U16)
+        nc.sync.dma_start(xt_w[:].bitcast(I32), xt_words[0].bitcast(I32))
+        l1 = load_list("l1", offs)
+        w_w = tile("w_w", [P, R], U32)
+        nc.sync.dma_start(w_w[:].bitcast(I32), w_words[0].rearrange("p n t -> p (n t)").bitcast(I32))
+        load_scale_halves(nc.sync, xt_stage, xt_scales)
+        load_scale_halves(nc.sync, w_stage, w_scales)
+        tb_rows = tb.rearrange("(p t) x -> t p x", t=PACK)
+        tbt = [tile(f"tb{t}", [P, X], F32) for t in range(PACK)]
+        nc.sync.dma_start(tbt[0][:], tb_rows[0])
+        l3 = load_list("l3", offs3)
+        l4 = load_list("l4", offs4)
+        l2 = load_list("l2", offs2)
+        nc.sync.dma_start(tbt[1][:], tb_rows[1])
+        l5 = load_list("l5", offs5)
+        nc.sync.dma_start(tbt[2][:], tb_rows[2])
+        load_scale_halves(nc.sync, out_stage[:, :, 0 : N // 4], ws_scales)
+        load_scale_halves(nc.sync, out_stage[:, :, N // 4 : 2 * N // 4], wb_scales)
+        nc.sync.dma_start(tbt[3][:], tb_rows[3])
+        ws_w = tile("ws_w", [P, N], U32)
+        nc.sync.dma_start(ws_w[:].bitcast(I32), ws_words[0].rearrange("p n t -> p (n t)").bitcast(I32))
+        wb_w = tile("wb_w", [P, N], U16)
+        nc.sync.dma_start(wb_w[:].bitcast(I32), wb_words[0].bitcast(I32))
+        l6 = load_list("l6", offs6)
+        l7 = load_list("l7", offs7)
+
+        g_w = tile("g_w", [P, J], U16)
+        nc.vector.tensor_copy(g_w[:], xt_w[:].indirect(l1[:]))
+        xt_plane = tile("xt_plane", [P, T // 4], I32)
+        for h in range(2):
+            nc.vector.tensor_copy(xt_plane[64 * h : 64 * (h + 1), :], xt_stage[:, h, :])
+        nc.vector.tensor_copy(w_stage[64:128, 0, :], w_stage[0:64, 1, :])
+        xt_bytes = xt_plane[:].bitcast(U8)
+        g_s = tile("g_s", [P, J], U8)
+        nc.vector.tensor_copy(g_s[:], xt_bytes.indirect(l1[:]))
+        w_dealt = tile("w_dealt", [P, PACK, P], U32)
+        nc.scalar.copy(w_dealt[:].rearrange("p t m -> p m t"), w_w[:].rearrange("p (m t) -> p m t", t=PACK))
+        w_plane = w_stage[:, 0, :].bitcast(U8).rearrange("p (m t) -> p t m", t=PACK)
+        w_sc = [tile(f"w_sc{t}", [P, P], U8) for t in range(PACK)]
+        a = [tile(f"a{t}", [P, J], F32) for t in range(PACK)]
+        picked = tile("picked", [P, PACK, O], F32)
+        upper = tile("upper", [P, PACK, O], F32)
+        lower = tile("lower", [P, PACK, O], F32)
+        cut = tile("cut", [P, PACK, O], F32)
+        for t in range(PACK):
+            nc.vector.tensor_copy(w_sc[t][:], w_plane[:, t, :])
+            a_ps = ps.tile([P, J], F32, name=f"a_ps{t}")
+            nc.tensor.matmul_mx(
+                out=a_ps[:], lhsT=w_dealt[:, t, :].bitcast(E4M3), lhsT_scale=w_sc[t][:],
+                rhs=g_w[:].bitcast(E2M1), rhs_scale=g_s[:], start=True, stop=True,
+            )
+            if t % 2 == 0:
+                nc.scalar.activation(a[t][:], a_ps[:], COPY)
+            else:
+                nc.vector.tensor_copy(a[t][:], a_ps[:])
+
+        nc.vector.tensor_copy(out_stage[64:128, 0, :], out_stage[0:64, 1, :])
+        out_plane = out_stage[:, 0, :].bitcast(U8)
+        g5_s = tile("g5_s", [P, O], U8)
+        nc.vector.tensor_copy(g5_s[:], xt_bytes.indirect(l5[:]))
+        g5_w = tile("g5_w", [P, O], U16)
+        nc.vector.tensor_copy(g5_w[:], xt_w[:].indirect(l5[:]))
+        p_ps = [ps.tile([P, O], F32, name=f"p_ps{h}") for h in range(2)]
+        for h in range(2):
+            nc.tensor.matmul_mx(
+                out=p_ps[h][:], lhsT=ws_w[:, P * h : P * (h + 1)].bitcast(E4M3), lhsT_scale=out_plane[:, P * h : P * (h + 1)],
+                rhs=g5_w[:].bitcast(E2M1), rhs_scale=g5_s[:], start=True, stop=False,
+            )
+
+        for t in range(PACK):
+            nc.vector.tensor_copy(picked[:, t, :], a[t][:].indirect(l2[:]))
+            nc.scalar.activation(upper[:, t, :], tbt[t][:].indirect(l3[:]), COPY, scale=a[t][:, LA_COL : LA_COL + 1])
+            nc.scalar.activation(lower[:, t, :], tbt[t][:].indirect(l4[:]), COPY, scale=a[t][:, LA2_COL : LA2_COL + 1])
+            nc.vector.tensor_tensor(cut[:, t, :], picked[:, t, :], upper[:, t, :], ALU.min)
+        hid = tile("hid", [P, O, PACK], BF16)
+        nc.vector.tensor_tensor(
+            hid[:].rearrange("p (c i) t -> p c t i", i=4),
+            cut[:].rearrange("p t (c i) -> p c t i", i=4),
+            lower[:].rearrange("p t (c i) -> p c t i", i=4),
+            ALU.max,
+        )
+        hid_w = tile("hid_w", [P, O], U32)
+        hid_s = tile("hid_s", [P, O], U8)
+        nc.vector.quantize_mx(out=hid_w[:].bitcast(E5M2), scales=hid_s[:], in_=hid[:].rearrange("p o t -> p (o t)"))
+
+        p = [tile(f"p{h}", [P, O], F32) for h in range(2)]
+        for h in range(2):
+            nc.tensor.matmul_mx(
+                out=p_ps[h][:], lhsT=wb_w[:, P * h : P * (h + 1)].bitcast(E2M1),
+                lhsT_scale=out_plane[:, N + P * h : N + P * (h + 1)],
+                rhs=hid_w[:].bitcast(E5M2), rhs_scale=hid_s[:], start=False, stop=True,
+            )
+        nc.vector.tensor_copy(p[0][:], p_ps[0][:])
+        nc.scalar.activation(p[1][:], p_ps[1][:], COPY)
+        for h in range(2):
+            nc.vector.tensor_copy(pages[0][h][:].indirect(l6[:]), p[h][:])
+            nc.scalar.activation(pages[1][h][:].indirect(l7[:]), p[h][:], COPY)
+        for h in range(2):
+            y = tile(f"y{h}", [P, E], F32)
+            nc.vector.tensor_tensor(y[:], pages[0][h][:], pages[1][h][:], ALU.add)
+            nc.sync.dma_start(out[P * h : P * (h + 1), :], y[:])

@@ -39,17 +39,23 @@ def tile_list_leadbounds_solo_further_pagetwice_kernel(
             nc.sync.dma_start(lst[:], src)
             return lst
 
-        def load_scale_halves(queue, dst, src):
+        def load_scale_rows(dst, src, first, q):
             rows = src[0].bitcast(I32).rearrange("(h q r) c -> q r h c", h=2, q=2)
-            for q in range(2):
-                queue.dma_start(dst[32 * q : 32 * q + 4], rows[q])
+            nc.sync.dma_start(dst[first + 32 * q : first + 32 * q + 4], rows[q])
+
+        def load_plane(queue, dst, src):
+            rows = src[0].bitcast(I32).rearrange("(q r) c -> r q c", r=4)
+            for r in range(4):
+                queue.dma_start(dst[r:P:32, :], rows[r])
 
         xt_stage = tile("xt_stage", [64, 2, T // 4], I32)
         w_stage = tile("w_stage", [P, 2, R // 4], I32)
-        out_stage = tile("out_stage", [P, 2, 2 * N // 4], I32)
-        nc.gpsimd.memset(xt_stage[:], 0)
-        nc.vector.memset(w_stage[:], 0)
-        nc.gpsimd.memset(out_stage[:], 0)
+        ws_plane = tile("ws_plane", [P, N // 4], I32)
+        wb_plane = tile("wb_plane", [P, N // 4], I32)
+        nc.vector.memset(xt_stage[:], 0)
+        nc.gpsimd.memset(w_stage[:], 0)
+        nc.gpsimd.memset(ws_plane[:], 0)
+        nc.vector.memset(wb_plane[:], 0)
         pages = [[tile(f"page{s}{h}", [P, E], F32) for h in range(2)] for s in range(2)]
         for s in range(2):
             for h in range(2):
@@ -58,101 +64,125 @@ def tile_list_leadbounds_solo_further_pagetwice_kernel(
         xt_w = tile("xt_w", [P, T], U16)
         nc.sync.dma_start(xt_w[:].bitcast(I32), xt_words[0].bitcast(I32))
         l1 = load_list("l1", offs)
+        for q in range(2):
+            load_scale_rows(xt_stage, xt_scales, 0, q)
+            load_scale_rows(w_stage, w_scales, 64, q)
         w_w = tile("w_w", [P, R], U32)
         nc.sync.dma_start(w_w[:].bitcast(I32), w_words[0].rearrange("p n t -> p (n t)").bitcast(I32))
-        load_scale_halves(nc.sync, xt_stage, xt_scales)
-        load_scale_halves(nc.sync, w_stage, w_scales)
         tb_rows = tb.rearrange("(p t) x -> t p x", t=PACK)
         tbt = [tile(f"tb{t}", [P, X], F32) for t in range(PACK)]
         nc.sync.dma_start(tbt[0][:], tb_rows[0])
         l3 = load_list("l3", offs3)
         l4 = load_list("l4", offs4)
-        l2 = load_list("l2", offs2)
-        nc.sync.dma_start(tbt[1][:], tb_rows[1])
         l5 = load_list("l5", offs5)
+        nc.sync.dma_start(tbt[1][:], tb_rows[1])
+        l2 = load_list("l2", offs2)
         nc.sync.dma_start(tbt[2][:], tb_rows[2])
-        load_scale_halves(nc.sync, out_stage[:, :, 0 : N // 4], ws_scales)
-        load_scale_halves(nc.sync, out_stage[:, :, N // 4 : 2 * N // 4], wb_scales)
         nc.sync.dma_start(tbt[3][:], tb_rows[3])
+        load_plane(nc.sync, wb_plane, wb_scales)
         ws_w = tile("ws_w", [P, N], U32)
         nc.sync.dma_start(ws_w[:].bitcast(I32), ws_words[0].rearrange("p n t -> p (n t)").bitcast(I32))
         wb_w = tile("wb_w", [P, N], U16)
         nc.sync.dma_start(wb_w[:].bitcast(I32), wb_words[0].bitcast(I32))
         l6 = load_list("l6", offs6)
         l7 = load_list("l7", offs7)
+        load_plane(nc.gpsimd, ws_plane, ws_scales)
 
         g_w = tile("g_w", [P, J], U16)
         nc.vector.tensor_copy(g_w[:], xt_w[:].indirect(l1[:]))
         xt_plane = tile("xt_plane", [P, T // 4], I32)
         for h in range(2):
             nc.vector.tensor_copy(xt_plane[64 * h : 64 * (h + 1), :], xt_stage[:, h, :])
-        nc.vector.tensor_copy(w_stage[64:128, 0, :], w_stage[0:64, 1, :])
+        nc.vector.tensor_copy(w_stage[0:64, 1, :], w_stage[64:128, 0, :])
         xt_bytes = xt_plane[:].bitcast(U8)
         g_s = tile("g_s", [P, J], U8)
         nc.vector.tensor_copy(g_s[:], xt_bytes.indirect(l1[:]))
-        w_dealt = tile("w_dealt", [P, PACK, P], U32)
-        nc.scalar.copy(w_dealt[:].rearrange("p t m -> p m t"), w_w[:].rearrange("p (m t) -> p m t", t=PACK))
-        w_plane = w_stage[:, 0, :].bitcast(U8).rearrange("p (m t) -> p t m", t=PACK)
-        w_sc = [tile(f"w_sc{t}", [P, P], U8) for t in range(PACK)]
+        w_cols = w_w[:].rearrange("p (m t) -> p m t", t=PACK)
+        w_first = tile("w_first", [P, P], U32)
+        w_rest = tile("w_rest", [P, PACK - 1, P], U32)
+        nc.scalar.copy(w_first[:], w_cols[:, :, 0])
+        nc.scalar.copy(w_rest[:].rearrange("p t m -> p m t"), w_cols[:, :, 1:PACK])
+        w_dealt = [w_first[:]] + [w_rest[:, t, :] for t in range(PACK - 1)]
+        w_plane = w_stage[:, 1, :].bitcast(U8).rearrange("p (m t) -> p t m", t=PACK)
+        w_sc0 = tile("w_sc0", [P, 1, P], U8)
+        w_sc1 = tile("w_sc1", [P, PACK - 1, P], U8)
+        nc.vector.tensor_copy(w_sc0[:], w_plane[:, 0:1, :])
+        nc.vector.tensor_copy(w_sc1[:], w_plane[:, 1:PACK, :])
+        w_sc = [w_sc0[:, 0, :]] + [w_sc1[:, t, :] for t in range(PACK - 1)]
         a = [tile(f"a{t}", [P, J], F32) for t in range(PACK)]
         picked = tile("picked", [P, PACK, O], F32)
         upper = tile("upper", [P, PACK, O], F32)
         lower = tile("lower", [P, PACK, O], F32)
         cut = tile("cut", [P, PACK, O], F32)
         for t in range(PACK):
-            nc.vector.tensor_copy(w_sc[t][:], w_plane[:, t, :])
             a_ps = ps.tile([P, J], F32, name=f"a_ps{t}")
             nc.tensor.matmul_mx(
-                out=a_ps[:], lhsT=w_dealt[:, t, :].bitcast(E4M3), lhsT_scale=w_sc[t][:],
+                out=a_ps[:], lhsT=w_dealt[t].bitcast(E4M3), lhsT_scale=w_sc[t],
                 rhs=g_w[:].bitcast(E2M1), rhs_scale=g_s[:], start=True, stop=True,
             )
-            if t % 2 == 0:
+            if t == 0:
                 nc.scalar.activation(a[t][:], a_ps[:], COPY)
             else:
                 nc.vector.tensor_copy(a[t][:], a_ps[:])
 
-        nc.vector.tensor_copy(out_stage[64:128, 0, :], out_stage[0:64, 1, :])
-        out_plane = out_stage[:, 0, :].bitcast(U8)
+        def bound(dst, t, lst, col, o0, o1):
+            nc.scalar.activation(
+                dst[:, t, o0:o1], tbt[t][:].indirect(lst[:, o0 // 16 : o1 // 16]), COPY, scale=a[t][:, col : col + 1]
+            )
+
+        last = PACK - 1
+        halves = ((0, O // 2), (O // 2, O))
+        for t in range(PACK):
+            nc.vector.tensor_copy(picked[:, t, :], a[t][:].indirect(l2[:]))
         g5_s = tile("g5_s", [P, O], U8)
         nc.vector.tensor_copy(g5_s[:], xt_bytes.indirect(l5[:]))
         g5_w = tile("g5_w", [P, O], U16)
         nc.vector.tensor_copy(g5_w[:], xt_w[:].indirect(l5[:]))
+        for t in range(last):
+            bound(upper, t, l3, LA_COL, 0, O)
+            bound(lower, t, l4, LA2_COL, 0, O)
+        nc.vector.tensor_tensor(cut[:, 0:last, :], picked[:, 0:last, :], upper[:, 0:last, :], ALU.min)
+        for o0, o1 in halves:
+            bound(upper, last, l3, LA_COL, o0, o1)
+            nc.vector.tensor_tensor(cut[:, last, o0:o1], picked[:, last, o0:o1], upper[:, last, o0:o1], ALU.min)
+        for o0, o1 in halves:
+            bound(lower, last, l4, LA2_COL, o0, o1)
         p_ps = [ps.tile([P, O], F32, name=f"p_ps{h}") for h in range(2)]
         for h in range(2):
             nc.tensor.matmul_mx(
-                out=p_ps[h][:], lhsT=ws_w[:, P * h : P * (h + 1)].bitcast(E4M3), lhsT_scale=out_plane[:, P * h : P * (h + 1)],
+                out=p_ps[h][:], lhsT=ws_w[:, P * h : P * (h + 1)].bitcast(E4M3), lhsT_scale=ws_plane[:].bitcast(U8)[:, P * h : P * (h + 1)],
                 rhs=g5_w[:].bitcast(E2M1), rhs_scale=g5_s[:], start=True, stop=False,
             )
-
-        for t in range(PACK):
-            nc.vector.tensor_copy(picked[:, t, :], a[t][:].indirect(l2[:]))
-            nc.scalar.activation(upper[:, t, :], tbt[t][:].indirect(l3[:]), COPY, scale=a[t][:, LA_COL : LA_COL + 1])
-            nc.scalar.activation(lower[:, t, :], tbt[t][:].indirect(l4[:]), COPY, scale=a[t][:, LA2_COL : LA2_COL + 1])
-            nc.vector.tensor_tensor(cut[:, t, :], picked[:, t, :], upper[:, t, :], ALU.min)
-        hid = tile("hid", [P, O, PACK], BF16)
-        nc.vector.tensor_tensor(
-            hid[:].rearrange("p (c i) t -> p c t i", i=4),
-            cut[:].rearrange("p t (c i) -> p c t i", i=4),
-            lower[:].rearrange("p t (c i) -> p c t i", i=4),
-            ALU.max,
-        )
+        hid = [tile(f"hid{k}", [P, O // 2, PACK], BF16) for k in range(2)]
+        for k, (o0, o1) in enumerate(halves):
+            nc.vector.tensor_tensor(
+                hid[k][:].rearrange("p (c i) t -> p c t i", i=4),
+                cut[:, :, o0:o1].rearrange("p t (c i) -> p c t i", i=4),
+                lower[:, :, o0:o1].rearrange("p t (c i) -> p c t i", i=4),
+                ALU.max,
+            )
         hid_w = tile("hid_w", [P, O], U32)
         hid_s = tile("hid_s", [P, O], U8)
-        nc.vector.quantize_mx(out=hid_w[:].bitcast(E5M2), scales=hid_s[:], in_=hid[:].rearrange("p o t -> p (o t)"))
+        for k, (o0, o1) in enumerate(halves):
+            nc.vector.quantize_mx(
+                out=hid_w[:, o0:o1].bitcast(E5M2), scales=hid_s[:, o0:o1], in_=hid[k][:].rearrange("p o t -> p (o t)")
+            )
 
         p = [tile(f"p{h}", [P, O], F32) for h in range(2)]
         for h in range(2):
             nc.tensor.matmul_mx(
                 out=p_ps[h][:], lhsT=wb_w[:, P * h : P * (h + 1)].bitcast(E2M1),
-                lhsT_scale=out_plane[:, N + P * h : N + P * (h + 1)],
+                lhsT_scale=wb_plane[:].bitcast(U8)[:, P * h : P * (h + 1)],
                 rhs=hid_w[:].bitcast(E5M2), rhs_scale=hid_s[:], start=False, stop=True,
             )
-        nc.vector.tensor_copy(p[0][:], p_ps[0][:])
-        nc.scalar.activation(p[1][:], p_ps[1][:], COPY)
+        for h in range(2):
+            nc.scalar.activation(p[h][:], p_ps[h][:], COPY)
         for h in range(2):
             nc.vector.tensor_copy(pages[0][h][:].indirect(l6[:]), p[h][:])
             nc.scalar.activation(pages[1][h][:].indirect(l7[:]), p[h][:], COPY)
         for h in range(2):
-            y = tile(f"y{h}", [P, E], F32)
-            nc.vector.tensor_tensor(y[:], pages[0][h][:], pages[1][h][:], ALU.add)
-            nc.sync.dma_start(out[P * h : P * (h + 1), :], y[:])
+            for c0 in range(0, E, E // 2):
+                c1 = c0 + E // 2
+                y = tile(f"y{h}_{c0}", [P, E // 2], F32)
+                nc.vector.tensor_tensor(y[:], pages[0][h][:, c0:c1], pages[1][h][:, c0:c1], ALU.add)
+                nc.sync.dma_start(out[P * h : P * (h + 1), c0:c1], y[:])

from contextlib import ExitStack

import concourse.mybir as mybir

K, T, J, R, X, O, N, E = 512, 1024, 256, 512, 1024, 128, 256, 512
FLOPS = 2 * K * R * J + 2 * R * N * O + 2 * K * N * O

F32 = mybir.dt.float32
BF16 = mybir.dt.bfloat16
I32 = mybir.dt.int32
U32 = mybir.dt.uint32
U16 = mybir.dt.uint16
U8 = mybir.dt.uint8
E4M3 = mybir.dt.float8_e4m3fn_x4
E5M2 = mybir.dt.float8_e5m2_x4
E2M1 = mybir.dt.float4_e2m1fn_x4
COPY = mybir.ActivationFunctionType.Copy
ALU = mybir.AluOpType

P = 128
PACK = 4
LA_COL, LA2_COL = 0, 128


def tile_list_leadbounds_solo_further_pagetwice_kernel(
    tc, xt_words, xt_scales, w_words, w_scales, tb, wb_words, wb_scales, ws_words, ws_scales,
    offs, offs2, offs3, offs4, offs5, offs6, offs7, out,
):
    nc = tc.nc
    with ExitStack() as ctx:
        sb = ctx.enter_context(tc.tile_pool(name="sb", bufs=1))
        ps = ctx.enter_context(tc.psum_pool(name="ps", bufs=1))

        def tile(name, shape, dtype):
            return sb.tile(shape, dtype, name=name, align_bytes=64)

        def load_list(name, src):
            lst = tile(name, list(src.shape), U16)
            nc.sync.dma_start(lst[:], src)
            return lst

        def load_scale_rows(dst, src, first, q):
            rows = src[0].bitcast(I32).rearrange("(h q r) c -> q r h c", h=2, q=2)
            nc.sync.dma_start(dst[first + 32 * q : first + 32 * q + 4], rows[q])

        def load_plane(queue, dst, src):
            rows = src[0].bitcast(I32).rearrange("(q r) c -> r q c", r=4)
            for r in range(4):
                queue.dma_start(dst[r:P:32, :], rows[r])

        xt_stage = tile("xt_stage", [64, 2, T // 4], I32)
        w_stage = tile("w_stage", [P, 2, R // 4], I32)
        ws_plane = tile("ws_plane", [P, N // 4], I32)
        wb_plane = tile("wb_plane", [P, N // 4], I32)
        nc.vector.memset(xt_stage[:], 0)
        nc.gpsimd.memset(w_stage[:], 0)
        nc.gpsimd.memset(ws_plane[:], 0)
        nc.vector.memset(wb_plane[:], 0)
        pages = [[tile(f"page{s}{h}", [P, E], F32) for h in range(2)] for s in range(2)]
        for s in range(2):
            for h in range(2):
                nc.vector.memset(pages[s][h][:], 0.0)

        xt_w = tile("xt_w", [P, T], U16)
        nc.sync.dma_start(xt_w[:].bitcast(I32), xt_words[0].bitcast(I32))
        l1 = load_list("l1", offs)
        for q in range(2):
            load_scale_rows(xt_stage, xt_scales, 0, q)
            load_scale_rows(w_stage, w_scales, 64, q)
        w_w = tile("w_w", [P, R], U32)
        nc.sync.dma_start(w_w[:].bitcast(I32), w_words[0].rearrange("p n t -> p (n t)").bitcast(I32))
        tb_rows = tb.rearrange("(p t) x -> t p x", t=PACK)
        tbt = [tile(f"tb{t}", [P, X], F32) for t in range(PACK)]
        nc.sync.dma_start(tbt[0][:], tb_rows[0])
        l3 = load_list("l3", offs3)
        l4 = load_list("l4", offs4)
        l5 = load_list("l5", offs5)
        nc.sync.dma_start(tbt[1][:], tb_rows[1])
        l2 = load_list("l2", offs2)
        nc.sync.dma_start(tbt[2][:], tb_rows[2])
        nc.sync.dma_start(tbt[3][:], tb_rows[3])
        load_plane(nc.sync, wb_plane, wb_scales)
        ws_w = tile("ws_w", [P, N], U32)
        nc.sync.dma_start(ws_w[:].bitcast(I32), ws_words[0].rearrange("p n t -> p (n t)").bitcast(I32))
        wb_w = tile("wb_w", [P, N], U16)
        nc.sync.dma_start(wb_w[:].bitcast(I32), wb_words[0].bitcast(I32))
        l6 = load_list("l6", offs6)
        l7 = load_list("l7", offs7)
        load_plane(nc.gpsimd, ws_plane, ws_scales)

        g_w = tile("g_w", [P, J], U16)
        nc.vector.tensor_copy(g_w[:], xt_w[:].indirect(l1[:]))
        xt_plane = tile("xt_plane", [P, T // 4], I32)
        for h in range(2):
            nc.vector.tensor_copy(xt_plane[64 * h : 64 * (h + 1), :], xt_stage[:, h, :])
        nc.vector.tensor_copy(w_stage[0:64, 1, :], w_stage[64:128, 0, :])
        xt_bytes = xt_plane[:].bitcast(U8)
        g_s = tile("g_s", [P, J], U8)
        nc.vector.tensor_copy(g_s[:], xt_bytes.indirect(l1[:]))
        w_cols = w_w[:].rearrange("p (m t) -> p m t", t=PACK)
        w_first = tile("w_first", [P, P], U32)
        w_rest = tile("w_rest", [P, PACK - 1, P], U32)
        nc.scalar.copy(w_first[:], w_cols[:, :, 0])
        nc.scalar.copy(w_rest[:].rearrange("p t m -> p m t"), w_cols[:, :, 1:PACK])
        w_dealt = [w_first[:]] + [w_rest[:, t, :] for t in range(PACK - 1)]
        w_plane = w_stage[:, 1, :].bitcast(U8).rearrange("p (m t) -> p t m", t=PACK)
        w_sc0 = tile("w_sc0", [P, 1, P], U8)
        w_sc1 = tile("w_sc1", [P, PACK - 1, P], U8)
        nc.vector.tensor_copy(w_sc0[:], w_plane[:, 0:1, :])
        nc.vector.tensor_copy(w_sc1[:], w_plane[:, 1:PACK, :])
        w_sc = [w_sc0[:, 0, :]] + [w_sc1[:, t, :] for t in range(PACK - 1)]
        a = [tile(f"a{t}", [P, J], F32) for t in range(PACK)]
        picked = tile("picked", [P, PACK, O], F32)
        upper = tile("upper", [P, PACK, O], F32)
        lower = tile("lower", [P, PACK, O], F32)
        cut = tile("cut", [P, PACK, O], F32)
        for t in range(PACK):
            a_ps = ps.tile([P, J], F32, name=f"a_ps{t}")
            nc.tensor.matmul_mx(
                out=a_ps[:], lhsT=w_dealt[t].bitcast(E4M3), lhsT_scale=w_sc[t],
                rhs=g_w[:].bitcast(E2M1), rhs_scale=g_s[:], start=True, stop=True,
            )
            if t == 0:
                nc.scalar.activation(a[t][:], a_ps[:], COPY)
            else:
                nc.vector.tensor_copy(a[t][:], a_ps[:])

        def bound(dst, t, lst, col, o0, o1):
            nc.scalar.activation(
                dst[:, t, o0:o1], tbt[t][:].indirect(lst[:, o0 // 16 : o1 // 16]), COPY, scale=a[t][:, col : col + 1]
            )

        last = PACK - 1
        halves = ((0, O // 2), (O // 2, O))
        for t in range(PACK):
            nc.vector.tensor_copy(picked[:, t, :], a[t][:].indirect(l2[:]))
        g5_s = tile("g5_s", [P, O], U8)
        nc.vector.tensor_copy(g5_s[:], xt_bytes.indirect(l5[:]))
        g5_w = tile("g5_w", [P, O], U16)
        nc.vector.tensor_copy(g5_w[:], xt_w[:].indirect(l5[:]))
        for t in range(last):
            bound(upper, t, l3, LA_COL, 0, O)
            bound(lower, t, l4, LA2_COL, 0, O)
        nc.vector.tensor_tensor(cut[:, 0:last, :], picked[:, 0:last, :], upper[:, 0:last, :], ALU.min)
        for o0, o1 in halves:
            bound(upper, last, l3, LA_COL, o0, o1)
            nc.vector.tensor_tensor(cut[:, last, o0:o1], picked[:, last, o0:o1], upper[:, last, o0:o1], ALU.min)
        for o0, o1 in halves:
            bound(lower, last, l4, LA2_COL, o0, o1)
        p_ps = [ps.tile([P, O], F32, name=f"p_ps{h}") for h in range(2)]
        for h in range(2):
            nc.tensor.matmul_mx(
                out=p_ps[h][:], lhsT=ws_w[:, P * h : P * (h + 1)].bitcast(E4M3), lhsT_scale=ws_plane[:].bitcast(U8)[:, P * h : P * (h + 1)],
                rhs=g5_w[:].bitcast(E2M1), rhs_scale=g5_s[:], start=True, stop=False,
            )
        hid = [tile(f"hid{k}", [P, O // 2, PACK], BF16) for k in range(2)]
        for k, (o0, o1) in enumerate(halves):
            nc.vector.tensor_tensor(
                hid[k][:].rearrange("p (c i) t -> p c t i", i=4),
                cut[:, :, o0:o1].rearrange("p t (c i) -> p c t i", i=4),
                lower[:, :, o0:o1].rearrange("p t (c i) -> p c t i", i=4),
                ALU.max,
            )
        hid_w = tile("hid_w", [P, O], U32)
        hid_s = tile("hid_s", [P, O], U8)
        for k, (o0, o1) in enumerate(halves):
            nc.vector.quantize_mx(
                out=hid_w[:, o0:o1].bitcast(E5M2), scales=hid_s[:, o0:o1], in_=hid[k][:].rearrange("p o t -> p (o t)")
            )

        p = [tile(f"p{h}", [P, O], F32) for h in range(2)]
        for h in range(2):
            nc.tensor.matmul_mx(
                out=p_ps[h][:], lhsT=wb_w[:, P * h : P * (h + 1)].bitcast(E2M1),
                lhsT_scale=wb_plane[:].bitcast(U8)[:, P * h : P * (h + 1)],
                rhs=hid_w[:].bitcast(E5M2), rhs_scale=hid_s[:], start=False, stop=True,
            )
        for h in range(2):
            nc.scalar.activation(p[h][:], p_ps[h][:], COPY)
        for h in range(2):
            nc.vector.tensor_copy(pages[0][h][:].indirect(l6[:]), p[h][:])
            nc.scalar.activation(pages[1][h][:].indirect(l7[:]), p[h][:], COPY)
        for h in range(2):
            for c0 in range(0, E, E // 2):
                c1 = c0 + E // 2
                y = tile(f"y{h}_{c0}", [P, E // 2], F32)
                nc.vector.tensor_tensor(y[:], pages[0][h][:, c0:c1], pages[1][h][:, c0:c1], ALU.add)
                nc.sync.dma_start(out[P * h : P * (h + 1), c0:c1], y[:])
